import numpy as np
import ml_dtypes


def mxq(x, axis, fmt="e4m3"):
    dtype, down = {"e4m3": (ml_dtypes.float8_e4m3fn, 7), "e5m2": (ml_dtypes.float8_e5m2, 14)}[fmt]
    v = np.moveaxis(np.asarray(x, np.float32).astype(ml_dtypes.bfloat16).astype(np.float64), axis, -1)
    blocks = v.reshape(v.shape[:-1] + (-1, 32))
    amax = np.abs(blocks).max(-1, keepdims=True)
    byte = np.maximum(np.where(amax > 0, np.frexp(amax)[1] - 1 + 127, 0) - down, 1)
    scale = np.exp2(byte - 127.0)
    codes = (blocks / scale).astype(np.float32).astype(dtype).astype(np.float64)
    return np.moveaxis((codes * scale).reshape(v.shape), -1, axis)


WIDE = False


def mx_kscale(k):
    if not WIDE:
        return np.ones(k)
    levels = np.array([18, -18])
    if k % 512:
        return np.exp2(np.random.permutation(np.resize(levels, k // 32))).repeat(32)
    a = np.empty((k // 512, 16))
    for p in range(k // 512):
        a[p, :8] = np.random.permutation(np.resize(levels, 8))
        for g in range(8):
            far = levels[np.abs(levels - a[p, g]) >= 10]
            a[p, g + 8] = far[np.random.randint(len(far))]
    return np.exp2(a.ravel()).repeat(32)


def f64(x):
    return np.asarray(x).astype(np.float64)


def striped(idx):
    return np.tile(np.asarray(idx).reshape(-1, 16).T, (8, 1)).astype(np.uint16)


def unstriped(offs):
    return offs[:16].T.reshape(-1).astype(np.int64)

def planes(y):
    n, m = y.shape
    v = y.astype(np.float32).astype(ml_dtypes.bfloat16).astype(np.float64).reshape(n // 32, 32, m)
    top = np.abs(v).max(1)
    byte = np.clip(np.where(top > 0, np.frexp(top)[1] - 1 + 127 - 7, 1), 1, 254)
    codes = (v * np.exp2(127.0 - byte)[:, None, :]).reshape(n, m).astype(np.float32).astype(ml_dtypes.float8_e4m3fn).view(np.uint8)
    words = codes.reshape(n // 512, 128, 4, m).transpose(0, 1, 3, 2)
    return np.ascontiguousarray(words), np.ascontiguousarray(byte.astype(np.uint8).reshape(n // 512, 16, m))


def setup_inputs():
    n = np.random.standard_normal
    uni = np.random.uniform
    idx = np.random.permutation(2048)[:512]
    f_d = mx_kscale(512)
    f_r = mx_kscale(512)
    return {
        "xT": (n((512, 512)) * f_d[:, None] * f_r[None, :]).astype(np.float32),
        "wT": (n((512, 2048)) / np.sqrt(512) / f_d[:, None]).astype(np.float32),
        "us": (uni(0.75, 1.3, (512, 1)) / f_r[:, None]).astype(np.float32),
        "fd": (uni(0.75, 1.3, (512, 1)) / f_d[:, None]).astype(np.float32),
        "offs": striped(idx),
    }


def reference(xT, wT, us, fd, offs):
    idx = unstriped(offs)
    w = f64(wT)[:, idx]
    a = mxq(f64(xT), 0, "e4m3").T @ mxq(w, 0, "e4m3")
    y = f64(us) * a
    g = f64(us) * y
    b = mxq(f64(xT), 1, "e4m3") @ mxq(g, 0, "e4m3")
    yt = y.T
    s = (np.square(yt)).sum(-1, keepdims=True)
    sr = s.T
    dw = np.square(f64(fd)) * b - sr * w
    out_0 = np.zeros((512, 2048))
    out_0[:, idx] = dw
    return (out_0,) + planes(out_0)

@@ -1,0 +1,255 @@
+from contextlib import ExitStack
+
+import concourse.mybir as mybir
+from concourse.masks import make_identity
+
+D, R, SLOTS, UNITS = 512, 512, 512, 2048
+FLOPS = 2 * 2 * D * R * SLOTS
+
+F32 = mybir.dt.float32
+BF16 = mybir.dt.bfloat16
+I32 = mybir.dt.int32
+U32 = mybir.dt.uint32
+U16 = mybir.dt.uint16
+U8 = mybir.dt.uint8
+FP8X4 = mybir.dt.float8_e4m3fn_x4
+MULT = mybir.AluOpType.mult
+ADD = mybir.AluOpType.add
+COPY = mybir.ActivationFunctionType.Copy
+SQUARE = mybir.ActivationFunctionType.Square
+
+P = 128
+LANES = 4
+HALF = SLOTS // 2
+QUARTER = SLOTS // 4
+CHUNK = 256
+STORE_COLS = 512
+SCALAR_WOVEN = 2
+
+
+def quantize(nc, codes, scales, values):
+    nc.vector.quantize_mx(out=codes.bitcast(FP8X4), scales=scales, in_=values)
+
+
+def product(nc, out, left, left_cols, right, right_cols):
+    nc.tensor.matmul_mx(
+        out=out,
+        lhsT=left[0][:, left_cols].bitcast(FP8X4),
+        lhsT_scale=left[1][:, left_cols],
+        rhs=right[0][:, right_cols].bitcast(FP8X4),
+        rhs_scale=right[1][:, right_cols],
+        start=True,
+        stop=True,
+    )
+
+
+def cols(index, width):
+    return slice(index * width, (index + 1) * width)
+
+
+def tile_attend_goja_pl_kernel(tc, xT, wT, us, fd, offs, out_0, out_1, out_2):
+    nc = tc.nc
+    with ExitStack() as ctx:
+        sb = ctx.enter_context(tc.tile_pool(name="sb", bufs=1))
+        ps = ctx.enter_context(tc.psum_pool(name="ps", bufs=1))
+
+        def operand(name, width):
+            return (
+                sb.tile([P, width], U32, name=name + "_codes", align_bytes=64),
+                sb.tile([P, width], U8, name=name + "_scales", align_bytes=64),
+            )
+
+        x_f32 = sb.tile([P, LANES, R], F32, name="x_f32")
+        nc.sync.dma_start(out=x_f32[:], in_=xT.rearrange("(p t) r -> p t r", t=LANES))
+        offsets = sb.tile([P, SLOTS // 16], U16, name="offsets")
+        nc.sync.dma_start(offsets[:], offs)
+        table = []
+        for t in range(LANES):
+            plane = sb.tile([P, UNITS], F32, name="table%d" % t)
+            nc.sync.dma_start(out=plane[:], in_=wT.rearrange("(p t) c -> p t c", t=LANES)[:, t, :])
+            table.append(plane)
+        us_col = sb.tile([P, LANES], F32, name="us_col")
+        nc.scalar.dma_start(out=us_col[:], in_=us.rearrange("(p t) o -> p (t o)", t=LANES))
+        fd_col = sb.tile([P, LANES], F32, name="fd_col")
+        nc.scalar.dma_start(out=fd_col[:], in_=fd.rearrange("(p t) o -> p (t o)", t=LANES))
+
+        ident = sb.tile([P, P], F32, name="ident")
+        make_identity(nc, ident[:])
+
+        moved = []
+        for t in range(LANES):
+            window = sb.tile([P, UNITS], F32, name="moved%d" % t)
+            nc.vector.memset(window[:], 0.0)
+            moved.append(window)
+
+        us_sq = sb.tile([P, LANES], F32, name="us_sq")
+        nc.scalar.activation(out=us_sq[:], in_=us_col[:], func=SQUARE)
+        fd_sq = sb.tile([P, LANES], F32, name="fd_sq")
+        nc.scalar.activation(out=fd_sq[:], in_=fd_col[:], func=SQUARE)
+
+        x_by_d = sb.tile([P, R * LANES], BF16, name="x_by_d", align_bytes=64)
+        nc.vector.tensor_copy(
+            out=x_by_d[:].rearrange("p (j s t) -> p s j t", j=LANES, t=LANES),
+            in_=x_f32[:].rearrange("p t (s j) -> p s j t", j=LANES),
+        )
+        xq_d = operand("xq_d", R)
+        quantize(nc, xq_d[0][:], xq_d[1][:], x_by_d[:])
+
+        x_bf16 = sb.tile([P, LANES * R], BF16, name="x_bf16")
+        nc.scalar.copy(out=x_bf16[:], in_=x_f32[:].rearrange("p t r -> p (t r)"))
+        x_words = x_bf16[:].bitcast(F32)
+        x_by_r = sb.tile([P, D * LANES], BF16, name="x_by_r", align_bytes=64)
+        x_by_r_words = x_by_r[:].bitcast(F32).rearrange("s (t p u) -> s t p u", t=LANES, u=2)
+        for h in range(2):
+            turned = ps.tile([P, 2, 2, P], F32, name="turned%d" % h, tag="turn%d" % h)
+            for tt in range(2):
+                t = 2 * h + tt
+                for u in range(2):
+                    nc.tensor.transpose(turned[:, tt, u, :], x_words[:, 256 * t + u : 256 * (t + 1) : 2], ident[:])
+            nc.scalar.copy(out=x_by_r_words[:, 2 * h : 2 * h + 2], in_=turned[:].rearrange("s t u p -> s t p u"))
+        xq_r = operand("xq_r", D)
+        quantize(nc, xq_r[0][:], xq_r[1][:], x_by_r[:])
+
+        w = sb.tile([P, LANES, SLOTS], F32, name="w")
+        w_bf16 = [sb.tile([P, HALF, LANES], BF16, name="w_bf16_%d" % h, align_bytes=64) for h in range(2)]
+        for t in range(LANES - 1):
+            nc.vector.tensor_copy(w[:, t, :], table[t][:].indirect(offsets[:]))
+            if t == 1:
+                for h in range(2):
+                    nc.scalar.copy(out=w_bf16[h][:, :, 0:2], in_=w[:, 0:2, cols(h, HALF)].rearrange("p t n -> p n t"))
+        for h in range(2):
+            nc.vector.tensor_copy(w[:, 3, cols(h, HALF)], table[3][:].indirect(offsets[:, cols(h, HALF // 16)]))
+        nc.scalar.copy(out=w_bf16[0][:, :, 2:4], in_=w[:, 2:4, cols(0, HALF)].rearrange("p t n -> p n t"))
+        nc.vector.tensor_copy(out=w_bf16[1][:, :, 2:4], in_=w[:, 2:4, cols(1, HALF)].rearrange("p t n -> p n t"))
+        wq = [operand("wq%d" % h, HALF) for h in range(2)]
+        for h in range(2):
+            quantize(nc, wq[h][0][:], wq[h][1][:], w_bf16[h][:].rearrange("p n t -> p (n t)"))
+
+        a = []
+        for q in range(4):
+            bank = ps.tile([P, LANES, QUARTER], F32, name="a%d" % q, tag="acc%d" % q)
+            for j in range(LANES):
+                product(nc, bank[:, j, :], xq_d, cols(j, P), wq[q // 2], cols(q % 2, QUARTER))
+            a.append(bank)
+
+        y_sq = [sb.tile([P, LANES, QUARTER], F32, name="y_sq%d" % q) for q in range(4)]
+        g_bf16 = [sb.tile([P, HALF * LANES], BF16, name="g_bf16_%d" % h, align_bytes=64) for h in range(2)]
+        gq = operand("gq", SLOTS)
+        y_sq_turned = ps.tile([P, 4, P], F32, name="y_sq_turned", tag="turn0")
+        neg_s = ps.tile([P, SLOTS], F32, name="neg_s", tag="turn1")
+        spent = sb.tile([P, P], F32, name="spent")
+        neg_s_col = [sb.tile([P, 1], F32, name="neg_s_col%d" % q) for q in range(4)]
+        b = [ps.tile([P, SLOTS], F32, name="b%d" % t, tag="b%d" % t) for t in range(2)]
+        hebb = [sb.tile([P, SLOTS], F32, name="hebb%d" % t) for t in range(LANES)]
+        decay = [sb.tile([P, SLOTS], F32, name="decay%d" % t) for t in range(LANES)]
+
+        def square(q):
+            for j in range(LANES):
+                nc.scalar.activation(out=y_sq[q][:, j, :], in_=a[q][:, j, :], func=SQUARE, scale=us_col[:, j : j + 1])
+
+        def make_g(q):
+            nc.vector.tensor_tensor(
+                out=g_bf16[q // 2][:, cols(q % 2, QUARTER * LANES)].rearrange("s (n j) -> s n j", j=LANES),
+                in0=a[q][:].rearrange("s j n -> s n j"),
+                in1=us_sq[:].unsqueeze(1).to_broadcast([P, QUARTER, LANES]),
+                op=MULT,
+            )
+
+        def turn_squares(q):
+            for j in range(LANES):
+                nc.tensor.matmul(
+                    y_sq_turned[:, q, :], y_sq[q][:, j, :], ident[:],
+                    start=(j == 0), stop=(j == LANES - 1), is_transpose=True,
+                )
+
+        def sum_squares(q):
+            nc.scalar.activation(out=spent[:], in_=y_sq_turned[:, q, :], func=COPY, scale=-1.0, accum_out=neg_s_col[q][:])
+
+        def spread(q):
+            nc.tensor.transpose(neg_s[:, cols(q, QUARTER)], neg_s_col[q][:].to_broadcast([P, P]), ident[:])
+
+        def scale_b(t, bank, span):
+            nc.scalar.activation(out=hebb[t][:, span], in_=bank[:, span], func=COPY, scale=fd_sq[:, t : t + 1])
+
+        def make_decay(t, span):
+            nc.vector.tensor_tensor(out=decay[t][:, span], in0=neg_s[:, span], in1=w[:, t, span], op=MULT)
+
+        def scatter(t, span):
+            lists = offsets[:, span.start // 16 : span.stop // 16]
+            nc.vector.tensor_tensor(moved[t][:].indirect(lists), hebb[t][:, span], decay[t][:, span], ADD)
+
+        for h in range(2):
+            span = cols(h, HALF)
+            for q in (2 * h, 2 * h + 1):
+                square(q)
+                make_g(q)
+            for q in (2 * h, 2 * h + 1):
+                turn_squares(q)
+            quantize(nc, gq[0][:, span], gq[1][:, span], g_bf16[h][:])
+            for q in (2 * h, 2 * h + 1):
+                sum_squares(q)
+            for q in (2 * h, 2 * h + 1):
+                spread(q)
+            product(nc, b[0][:, span], xq_r, cols(0, P), gq, span)
+            scale_b(0, b[0], span)
+            if h == 0:
+                make_decay(0, span)
+                scatter(0, span)
+
+        whole = slice(0, SLOTS)
+        for t in range(1, LANES):
+            if t > 1:
+                b.append(ps.tile([P, SLOTS], F32, name="b%d" % t, tag="acc%d" % (t - 2)))
+            product(nc, b[t][:], xq_r, cols(t, P), gq, whole)
+            scale_b(t, b[t], whole)
+
+        chunks = UNITS // CHUNK
+        pairs = [sb.tile([P, 2, CHUNK, 2], BF16, name="pairs%d" % k) for k in range(chunks)]
+        out_rows = out_0.rearrange("(p t) c -> p t c", t=LANES)
+
+        def finish_plane(t):
+            nc.sync.dma_start(out=out_rows[:, t, :], in_=moved[t][:])
+            for k in range(chunks):
+                nc.scalar.copy(out=pairs[k][:, t // 2, :, t % 2], in_=moved[t][:, cols(k, CHUNK)])
+
+        make_decay(0, cols(1, HALF))
+        make_decay(1, whole)
+        scatter(0, cols(1, HALF))
+        finish_plane(0)
+        for t in range(1, LANES):
+            if t + 1 < LANES:
+                make_decay(t + 1, whole)
+            scatter(t, whole)
+            finish_plane(t)
+
+        y_scales = sb.tile([P, UNITS], U8, name="y_scales", align_bytes=64)
+        y_codes = [sb.tile([P, STORE_COLS], U32, name="y_codes%d" % m, align_bytes=64) for m in range(UNITS // STORE_COLS)]
+        woven = [sb.tile([P, CHUNK * LANES], BF16, name="woven%d" % k, align_bytes=64) for k in range(chunks)]
+        out_words = out_1[0].rearrange("p c l -> p (c l)").bitcast(I32)
+        per_store = STORE_COLS // CHUNK
+
+        def weave(k):
+            if k >= chunks - SCALAR_WOVEN:
+                nc.scalar.copy(
+                    out=woven[k][:].bitcast(U32).rearrange("p (c u) -> p c u", u=2),
+                    in_=pairs[k][:].rearrange("p u c e -> p (u c e)").bitcast(U32).rearrange("p (u c) -> p c u", u=2),
+                )
+            else:
+                nc.vector.tensor_copy(
+                    out=woven[k][:].bitcast(I32).rearrange("p (c u) -> p c u", u=2),
+                    in_=pairs[k][:].rearrange("p u c e -> p (u c e)").bitcast(I32).rearrange("p (u c) -> p c u", u=2),
+                )
+
+        weave(0)
+        for k in range(chunks):
+            if k + 1 < chunks:
+                weave(k + 1)
+            m = k // per_store
+            quantize(nc, y_codes[m][:, cols(k % per_store, CHUNK)], y_scales[:, cols(k, CHUNK)], woven[k][:])
+            if k % per_store == per_store - 1:
+                nc.sync.dma_start(out=out_words[:, cols(m, STORE_COLS)], in_=y_codes[m][:].bitcast(I32))
+        for quad in range(4):
+            nc.scalar.dma_start(
+                out=out_2[0, 4 * quad : 4 * quad + 4, :].bitcast(I32),
+                in_=y_scales[32 * quad : 32 * quad + 4, :].bitcast(I32),
+            )

@@ -22,8 +22,7 @@ P = 128
 LANES = 4
 HALF = SLOTS // 2
 QUARTER = SLOTS // 4
-CHUNK = 256
-STORE_COLS = 512
+CHUNKS = ((256, 256), (256, 256), (256, 256), (256,), (256,))
 SCALAR_WOVEN = 2
 
 
@@ -79,7 +78,7 @@ def tile_attend_goja_pl_kernel(tc, xT, wT, us, fd, offs, out_0, out_1, out_2):
         moved = []
         for t in range(LANES):
             window = sb.tile([P, UNITS], F32, name="moved%d" % t)
-            nc.vector.memset(window[:], 0.0)
+            (nc.gpsimd if t >= 2 else nc.vector).memset(window[:], 0.0)
             moved.append(window)
 
         us_sq = sb.tile([P, LANES], F32, name="us_sq")
@@ -110,18 +109,17 @@ def tile_attend_goja_pl_kernel(tc, xT, wT, us, fd, offs, out_0, out_1, out_2):
         xq_r = operand("xq_r", D)
         quantize(nc, xq_r[0][:], xq_r[1][:], x_by_r[:])
 
-        w = sb.tile([P, LANES, SLOTS], F32, name="w")
+        w = [sb.tile([P, LANES, HALF], F32, name="w%d" % h) for h in range(2)]
         w_bf16 = [sb.tile([P, HALF, LANES], BF16, name="w_bf16_%d" % h, align_bytes=64) for h in range(2)]
-        for t in range(LANES - 1):
-            nc.vector.tensor_copy(w[:, t, :], table[t][:].indirect(offsets[:]))
+        wq = [operand("wq%d" % h, HALF) for h in range(2)]
+        for t in range(LANES):
+            for h in range(2):
+                nc.vector.tensor_copy(w[h][:, t, :], table[t][:].indirect(offsets[:, cols(h, HALF // 16)]))
             if t == 1:
                 for h in range(2):
-                    nc.scalar.copy(out=w_bf16[h][:, :, 0:2], in_=w[:, 0:2, cols(h, HALF)].rearrange("p t n -> p n t"))
-        for h in range(2):
-            nc.vector.tensor_copy(w[:, 3, cols(h, HALF)], table[3][:].indirect(offsets[:, cols(h, HALF // 16)]))
-        nc.scalar.copy(out=w_bf16[0][:, :, 2:4], in_=w[:, 2:4, cols(0, HALF)].rearrange("p t n -> p n t"))
-        nc.vector.tensor_copy(out=w_bf16[1][:, :, 2:4], in_=w[:, 2:4, cols(1, HALF)].rearrange("p t n -> p n t"))
-        wq = [operand("wq%d" % h, HALF) for h in range(2)]
+                    nc.scalar.copy(out=w_bf16[h][:, :, 0:2], in_=w[h][:, 0:2, :].rearrange("p t n -> p n t"))
+        nc.scalar.copy(out=w_bf16[0][:, :, 2:4], in_=w[0][:, 2:4, :].rearrange("p t n -> p n t"))
+        nc.vector.tensor_copy(out=w_bf16[1][:, :, 2:4], in_=w[1][:, 2:4, :].rearrange("p t n -> p n t"))
         for h in range(2):
             quantize(nc, wq[h][0][:], wq[h][1][:], w_bf16[h][:].rearrange("p n t -> p (n t)"))
 
@@ -135,13 +133,12 @@ def tile_attend_goja_pl_kernel(tc, xT, wT, us, fd, offs, out_0, out_1, out_2):
         y_sq = [sb.tile([P, LANES, QUARTER], F32, name="y_sq%d" % q) for q in range(4)]
         g_bf16 = [sb.tile([P, HALF * LANES], BF16, name="g_bf16_%d" % h, align_bytes=64) for h in range(2)]
         gq = operand("gq", SLOTS)
-        y_sq_turned = ps.tile([P, 4, P], F32, name="y_sq_turned", tag="turn0")
-        neg_s = ps.tile([P, SLOTS], F32, name="neg_s", tag="turn1")
+        sums = [ps.tile([P, 2, HALF], F32, name="sums%d" % h, tag="turn%d" % h) for h in range(2)]
         spent = sb.tile([P, P], F32, name="spent")
-        neg_s_col = [sb.tile([P, 1], F32, name="neg_s_col%d" % q) for q in range(4)]
+        s_cols = [sb.tile([P, 2], F32, name="s_cols%d" % h) for h in range(2)]
         b = [ps.tile([P, SLOTS], F32, name="b%d" % t, tag="b%d" % t) for t in range(2)]
         hebb = [sb.tile([P, SLOTS], F32, name="hebb%d" % t) for t in range(LANES)]
-        decay = [sb.tile([P, SLOTS], F32, name="decay%d" % t) for t in range(LANES)]
+        decay = sb.tile([P, LANES, SLOTS], F32, name="decay")
 
         def square(q):
             for j in range(LANES):
@@ -158,78 +155,97 @@ def tile_attend_goja_pl_kernel(tc, xT, wT, us, fd, offs, out_0, out_1, out_2):
         def turn_squares(q):
             for j in range(LANES):
                 nc.tensor.matmul(
-                    y_sq_turned[:, q, :], y_sq[q][:, j, :], ident[:],
+                    sums[q // 2][:, 0, cols(q % 2, P)], y_sq[q][:, j, :], ident[:],
                     start=(j == 0), stop=(j == LANES - 1), is_transpose=True,
                 )
 
-        def sum_squares(q):
-            nc.scalar.activation(out=spent[:], in_=y_sq_turned[:, q, :], func=COPY, scale=-1.0, accum_out=neg_s_col[q][:])
+        def sum_squares(h):
+            for k in range(2):
+                nc.scalar.activation(
+                    out=spent[:], in_=sums[h][:, 0, cols(k, P)], func=COPY, accum_out=s_cols[h][:, k : k + 1]
+                )
 
         def spread(q):
-            nc.tensor.transpose(neg_s[:, cols(q, QUARTER)], neg_s_col[q][:].to_broadcast([P, P]), ident[:])
+            column = s_cols[q // 2][:, q % 2 : q % 2 + 1]
+            nc.tensor.transpose(sums[q // 2][:, 1, cols(q % 2, QUARTER)], column.to_broadcast([P, P]), ident[:])
 
         def scale_b(t, bank, span):
             nc.scalar.activation(out=hebb[t][:, span], in_=bank[:, span], func=COPY, scale=fd_sq[:, t : t + 1])
 
-        def make_decay(t, span):
-            nc.vector.tensor_tensor(out=decay[t][:, span], in0=neg_s[:, span], in1=w[:, t, span], op=MULT)
+        def make_decay(planes, h):
+            count = planes.stop - planes.start
+            nc.vector.scalar_tensor_tensor(
+                out=decay[:, planes, cols(h, HALF)],
+                in0=sums[h][:, 1:2, :].to_broadcast([P, count, HALF]),
+                scalar=-1.0,
+                in1=w[h][:, planes, :],
+                op0=MULT,
+                op1=MULT,
+            )
 
         def scatter(t, span):
             lists = offsets[:, span.start // 16 : span.stop // 16]
-            nc.vector.tensor_tensor(moved[t][:].indirect(lists), hebb[t][:, span], decay[t][:, span], ADD)
+            nc.vector.tensor_tensor(moved[t][:].indirect(lists), hebb[t][:, span], decay[:, t, span], ADD)
 
-        for h in range(2):
-            span = cols(h, HALF)
-            for q in (2 * h, 2 * h + 1):
-                square(q)
-                make_g(q)
-            for q in (2 * h, 2 * h + 1):
-                turn_squares(q)
-            quantize(nc, gq[0][:, span], gq[1][:, span], g_bf16[h][:])
-            for q in (2 * h, 2 * h + 1):
-                sum_squares(q)
-            for q in (2 * h, 2 * h + 1):
-                spread(q)
-            product(nc, b[0][:, span], xq_r, cols(0, P), gq, span)
-            scale_b(0, b[0], span)
-            if h == 0:
-                make_decay(0, span)
-                scatter(0, span)
+        first, second = cols(0, HALF), cols(1, HALF)
+        make_g(0)
+        square(1)
+        square(0)
+        make_g(2)
+        make_g(1)
+        turn_squares(1)
+        turn_squares(0)
+        make_g(3)
+        quantize(nc, gq[0][:, first], gq[1][:, first], g_bf16[0][:])
+        sum_squares(0)
+        product(nc, b[0][:, first], xq_r, cols(0, P), gq, first)
+        for q in (0, 1):
+            spread(q)
+        scale_b(0, b[0], first)
+        quantize(nc, gq[0][:, second], gq[1][:, second], g_bf16[1][:])
+        make_decay(slice(0, 1), 0)
+        for q in (2, 3):
+            square(q)
+            turn_squares(q)
+        scatter(0, first)
+        make_decay(slice(1, LANES), 0)
+        sum_squares(1)
+        product(nc, b[0][:, second], xq_r, cols(0, P), gq, second)
+        scale_b(0, b[0], second)
+        for q in (2, 3):
+            spread(q)
 
         whole = slice(0, SLOTS)
         for t in range(1, LANES):
             if t > 1:
-                b.append(ps.tile([P, SLOTS], F32, name="b%d" % t, tag="acc%d" % (t - 2)))
+                b.append(ps.tile([P, SLOTS], F32, name="b%d" % t, tag="acc%d" % t))
             product(nc, b[t][:], xq_r, cols(t, P), gq, whole)
             scale_b(t, b[t], whole)
 
-        chunks = UNITS // CHUNK
-        pairs = [sb.tile([P, 2, CHUNK, 2], BF16, name="pairs%d" % k) for k in range(chunks)]
+        widths = [width for group in CHUNKS for width in group]
+        spans = [slice(sum(widths[:k]), sum(widths[: k + 1])) for k in range(len(widths))]
+        pairs = [sb.tile([P, 2, width, 2], BF16, name="pairs%d" % k) for k, width in enumerate(widths)]
         out_rows = out_0.rearrange("(p t) c -> p t c", t=LANES)
 
         def finish_plane(t):
             nc.sync.dma_start(out=out_rows[:, t, :], in_=moved[t][:])
-            for k in range(chunks):
-                nc.scalar.copy(out=pairs[k][:, t // 2, :, t % 2], in_=moved[t][:, cols(k, CHUNK)])
+            for k, span in enumerate(spans):
+                nc.scalar.copy(out=pairs[k][:, t // 2, :, t % 2], in_=moved[t][:, span])
 
-        make_decay(0, cols(1, HALF))
-        make_decay(1, whole)
-        scatter(0, cols(1, HALF))
-        finish_plane(0)
-        for t in range(1, LANES):
+        make_decay(slice(0, 1), 1)
+        for t in range(LANES):
             if t + 1 < LANES:
-                make_decay(t + 1, whole)
-            scatter(t, whole)
+                make_decay(slice(t + 1, t + 2), 1)
+            scatter(t, second if t == 0 else whole)
             finish_plane(t)
 
         y_scales = sb.tile([P, UNITS], U8, name="y_scales", align_bytes=64)
-        y_codes = [sb.tile([P, STORE_COLS], U32, name="y_codes%d" % m, align_bytes=64) for m in range(UNITS // STORE_COLS)]
-        woven = [sb.tile([P, CHUNK * LANES], BF16, name="woven%d" % k, align_bytes=64) for k in range(chunks)]
+        y_codes = [sb.tile([P, sum(group)], U32, name="y_codes%d" % m, align_bytes=64) for m, group in enumerate(CHUNKS)]
+        woven = [sb.tile([P, width * LANES], BF16, name="woven%d" % k, align_bytes=64) for k, width in enumerate(widths)]
         out_words = out_1[0].rearrange("p c l -> p (c l)").bitcast(I32)
-        per_store = STORE_COLS // CHUNK
 
         def weave(k):
-            if k >= chunks - SCALAR_WOVEN:
+            if k >= len(widths) - SCALAR_WOVEN:
                 nc.scalar.copy(
                     out=woven[k][:].bitcast(U32).rearrange("p (c u) -> p c u", u=2),
                     in_=pairs[k][:].rearrange("p u c e -> p (u c e)").bitcast(U32).rearrange("p (u c) -> p c u", u=2),
@@ -241,15 +257,18 @@ def tile_attend_goja_pl_kernel(tc, xT, wT, us, fd, offs, out_0, out_1, out_2):
                 )
 
         weave(0)
-        for k in range(chunks):
-            if k + 1 < chunks:
-                weave(k + 1)
-            m = k // per_store
-            quantize(nc, y_codes[m][:, cols(k % per_store, CHUNK)], y_scales[:, cols(k, CHUNK)], woven[k][:])
-            if k % per_store == per_store - 1:
-                nc.sync.dma_start(out=out_words[:, cols(m, STORE_COLS)], in_=y_codes[m][:].bitcast(I32))
+        k = 0
+        for m, group in enumerate(CHUNKS):
+            base = spans[k].start
+            for width in group:
+                if k + 1 < len(widths):
+                    weave(k + 1)
+                start = spans[k].start - base
+                quantize(nc, y_codes[m][:, start : start + width], y_scales[:, spans[k]], woven[k][:])
+                k = k + 1
+            nc.sync.dma_start(out=out_words[:, base : base + sum(group)], in_=y_codes[m][:].bitcast(I32))
         for quad in range(4):
-            nc.scalar.dma_start(
+            (nc.scalar if quad < 2 else nc.sync).dma_start(
                 out=out_2[0, 4 * quad : 4 * quad + 4, :].bitcast(I32),
                 in_=y_scales[32 * quad : 32 * quad + 4, :].bitcast(I32),
             )

@@ -22,7 +22,7 @@ P = 128
 LANES = 4
 HALF = SLOTS // 2
 QUARTER = SLOTS // 4
-CHUNKS = ((256, 256), (256, 256), (256, 256), (256,), (256,))
+CHUNKS = ((128, 128, 256), (256, 256), (256, 256), (256,), (256,))
 SCALAR_WOVEN = 2
 
 
@@ -78,7 +78,7 @@ def tile_attend_goja_pl_kernel(tc, xT, wT, us, fd, offs, out_0, out_1, out_2):
         moved = []
         for t in range(LANES):
             window = sb.tile([P, UNITS], F32, name="moved%d" % t)
-            (nc.gpsimd if t >= 2 else nc.vector).memset(window[:], 0.0)
+            nc.vector.memset(window[:], 0.0)
             moved.append(window)
 
         us_sq = sb.tile([P, LANES], F32, name="us_sq")
@@ -92,7 +92,6 @@ def tile_attend_goja_pl_kernel(tc, xT, wT, us, fd, offs, out_0, out_1, out_2):
             in_=x_f32[:].rearrange("p t (s j) -> p s j t", j=LANES),
         )
         xq_d = operand("xq_d", R)
-        quantize(nc, xq_d[0][:], xq_d[1][:], x_by_d[:])
 
         x_bf16 = sb.tile([P, LANES * R], BF16, name="x_bf16")
         nc.scalar.copy(out=x_bf16[:], in_=x_f32[:].rearrange("p t r -> p (t r)"))
@@ -107,7 +106,6 @@ def tile_attend_goja_pl_kernel(tc, xT, wT, us, fd, offs, out_0, out_1, out_2):
                     nc.tensor.transpose(turned[:, tt, u, :], x_words[:, 256 * t + u : 256 * (t + 1) : 2], ident[:])
             nc.scalar.copy(out=x_by_r_words[:, 2 * h : 2 * h + 2], in_=turned[:].rearrange("s t u p -> s t p u"))
         xq_r = operand("xq_r", D)
-        quantize(nc, xq_r[0][:], xq_r[1][:], x_by_r[:])
 
         w = [sb.tile([P, LANES, HALF], F32, name="w%d" % h) for h in range(2)]
         w_bf16 = [sb.tile([P, HALF, LANES], BF16, name="w_bf16_%d" % h, align_bytes=64) for h in range(2)]
@@ -115,7 +113,10 @@ def tile_attend_goja_pl_kernel(tc, xT, wT, us, fd, offs, out_0, out_1, out_2):
         for t in range(LANES):
             for h in range(2):
                 nc.vector.tensor_copy(w[h][:, t, :], table[t][:].indirect(offsets[:, cols(h, HALF // 16)]))
+            if t == 0:
+                quantize(nc, xq_d[0][:], xq_d[1][:], x_by_d[:])
             if t == 1:
+                quantize(nc, xq_r[0][:], xq_r[1][:], x_by_r[:])
                 for h in range(2):
                     nc.scalar.copy(out=w_bf16[h][:, :, 0:2], in_=w[h][:, 0:2, :].rearrange("p t n -> p n t"))
         nc.scalar.copy(out=w_bf16[0][:, :, 2:4], in_=w[0][:, 2:4, :].rearrange("p t n -> p n t"))
@@ -134,7 +135,7 @@ def tile_attend_goja_pl_kernel(tc, xT, wT, us, fd, offs, out_0, out_1, out_2):
         g_bf16 = [sb.tile([P, HALF * LANES], BF16, name="g_bf16_%d" % h, align_bytes=64) for h in range(2)]
         gq = operand("gq", SLOTS)
         sums = [ps.tile([P, 2, HALF], F32, name="sums%d" % h, tag="turn%d" % h) for h in range(2)]
-        spent = sb.tile([P, P], F32, name="spent")
+        spent = sb.tile([P, SLOTS], F32, name="spent")
         s_cols = [sb.tile([P, 2], F32, name="s_cols%d" % h) for h in range(2)]
         b = [ps.tile([P, SLOTS], F32, name="b%d" % t, tag="b%d" % t) for t in range(2)]
         hebb = [sb.tile([P, SLOTS], F32, name="hebb%d" % t) for t in range(LANES)]
@@ -162,7 +163,7 @@ def tile_attend_goja_pl_kernel(tc, xT, wT, us, fd, offs, out_0, out_1, out_2):
         def sum_squares(h):
             for k in range(2):
                 nc.scalar.activation(
-                    out=spent[:], in_=sums[h][:, 0, cols(k, P)], func=COPY, accum_out=s_cols[h][:, k : k + 1]
+                    out=spent[:, cols(2 * h + k, P)], in_=sums[h][:, 0, cols(k, P)], func=COPY, accum_out=s_cols[h][:, k : k + 1]
                 )
 
         def spread(q):
@@ -208,7 +209,7 @@ def tile_attend_goja_pl_kernel(tc, xT, wT, us, fd, offs, out_0, out_1, out_2):
             square(q)
             turn_squares(q)
         scatter(0, first)
-        make_decay(slice(1, LANES), 0)
+        make_decay(slice(1, 2), 0)
         sum_squares(1)
         product(nc, b[0][:, second], xq_r, cols(0, P), gq, second)
         scale_b(0, b[0], second)
@@ -232,10 +233,11 @@ def tile_attend_goja_pl_kernel(tc, xT, wT, us, fd, offs, out_0, out_1, out_2):
             for k, span in enumerate(spans):
                 nc.scalar.copy(out=pairs[k][:, t // 2, :, t % 2], in_=moved[t][:, span])
 
-        make_decay(slice(0, 1), 1)
+        make_decay(slice(0, 2), 1)
         for t in range(LANES):
-            if t + 1 < LANES:
-                make_decay(slice(t + 1, t + 2), 1)
+            if 0 < t < LANES - 1:
+                for h in range(2):
+                    make_decay(slice(t + 1, t + 2), h)
             scatter(t, second if t == 0 else whole)
             finish_plane(t)
 
@@ -247,13 +249,20 @@ def tile_attend_goja_pl_kernel(tc, xT, wT, us, fd, offs, out_0, out_1, out_2):
         def weave(k):
             if k >= len(widths) - SCALAR_WOVEN:
                 nc.scalar.copy(
-                    out=woven[k][:].bitcast(U32).rearrange("p (c u) -> p c u", u=2),
-                    in_=pairs[k][:].rearrange("p u c e -> p (u c e)").bitcast(U32).rearrange("p (u c) -> p c u", u=2),
+                    out=woven[k][:].bitcast(U32).rearrange("p (c i u) -> p c u i", i=2, u=2),
+                    in_=pairs[k][:].rearrange("p u c e -> p (u c e)").bitcast(U32).rearrange("p (u c i) -> p c u i", u=2, i=2),
                 )
             else:
                 nc.vector.tensor_copy(
-                    out=woven[k][:].bitcast(I32).rearrange("p (c u) -> p c u", u=2),
-                    in_=pairs[k][:].rearrange("p u c e -> p (u c e)").bitcast(I32).rearrange("p (u c) -> p c u", u=2),
+                    out=woven[k][:].bitcast(I32).rearrange("p (c i u) -> p c u i", i=2, u=2),
+                    in_=pairs[k][:].rearrange("p u c e -> p (u c e)").bitcast(I32).rearrange("p (u c i) -> p c u i", u=2, i=2),
+                )
+
+        def store_scales(span, queues):
+            for quad in range(4):
+                queues[quad % len(queues)].dma_start(
+                    out=out_2[0, 4 * quad : 4 * quad + 4, span].bitcast(I32),
+                    in_=y_scales[32 * quad : 32 * quad + 4, span].bitcast(I32),
                 )
 
         weave(0)
@@ -267,8 +276,4 @@ def tile_attend_goja_pl_kernel(tc, xT, wT, us, fd, offs, out_0, out_1, out_2):
                 quantize(nc, y_codes[m][:, start : start + width], y_scales[:, spans[k]], woven[k][:])
                 k = k + 1
             nc.sync.dma_start(out=out_words[:, base : base + sum(group)], in_=y_codes[m][:].bitcast(I32))
-        for quad in range(4):
-            (nc.scalar if quad < 2 else nc.sync).dma_start(
-                out=out_2[0, 4 * quad : 4 * quad + 4, :].bitcast(I32),
-                in_=y_scales[32 * quad : 32 * quad + 4, :].bitcast(I32),
-            )
+        store_scales(slice(0, UNITS), [nc.scalar, nc.sync])

@@ -22,7 +22,7 @@ P = 128
 LANES = 4
 HALF = SLOTS // 2
 QUARTER = SLOTS // 4
-CHUNKS = ((128, 128, 256), (256, 256), (256, 256), (256,), (256,))
+CHUNKS = ((128, 128, 256), (256, 256), (256, 256), (128, 256), (128,))
 SCALAR_WOVEN = 2
 
 
@@ -108,8 +108,18 @@ def tile_attend_goja_pl_kernel(tc, xT, wT, us, fd, offs, out_0, out_1, out_2):
         xq_r = operand("xq_r", D)
 
         w = [sb.tile([P, LANES, HALF], F32, name="w%d" % h) for h in range(2)]
-        w_bf16 = [sb.tile([P, HALF, LANES], BF16, name="w_bf16_%d" % h, align_bytes=64) for h in range(2)]
-        wq = [operand("wq%d" % h, HALF) for h in range(2)]
+        pieces = (cols(0, QUARTER), cols(1, QUARTER), cols(1, HALF))
+        w_bf16 = [
+            sb.tile([P, piece.stop - piece.start, LANES], BF16, name="w_bf16_%d" % k, align_bytes=64)
+            for k, piece in enumerate(pieces)
+        ]
+        wq = [operand("wq%d" % k, piece.stop - piece.start) for k, piece in enumerate(pieces)]
+
+        def round_w(copy, k, lanes):
+            h = pieces[k].start // HALF
+            inside = slice(pieces[k].start - h * HALF, pieces[k].stop - h * HALF)
+            copy(out=w_bf16[k][:, :, lanes], in_=w[h][:, lanes, inside].rearrange("p t n -> p n t"))
+
         for t in range(LANES):
             for h in range(2):
                 nc.vector.tensor_copy(w[h][:, t, :], table[t][:].indirect(offsets[:, cols(h, HALF // 16)]))
@@ -117,27 +127,29 @@ def tile_attend_goja_pl_kernel(tc, xT, wT, us, fd, offs, out_0, out_1, out_2):
                 quantize(nc, xq_d[0][:], xq_d[1][:], x_by_d[:])
             if t == 1:
                 quantize(nc, xq_r[0][:], xq_r[1][:], x_by_r[:])
-                for h in range(2):
-                    nc.scalar.copy(out=w_bf16[h][:, :, 0:2], in_=w[h][:, 0:2, :].rearrange("p t n -> p n t"))
-        nc.scalar.copy(out=w_bf16[0][:, :, 2:4], in_=w[0][:, 2:4, :].rearrange("p t n -> p n t"))
-        nc.vector.tensor_copy(out=w_bf16[1][:, :, 2:4], in_=w[1][:, 2:4, :].rearrange("p t n -> p n t"))
-        for h in range(2):
-            quantize(nc, wq[h][0][:], wq[h][1][:], w_bf16[h][:].rearrange("p n t -> p (n t)"))
+                for k in range(len(pieces)):
+                    round_w(nc.scalar.copy, k, slice(0, 2))
+        for k in range(len(pieces)):
+            round_w(nc.scalar.copy if k < 2 else nc.vector.tensor_copy, k, slice(2, 4))
+            quantize(nc, wq[k][0][:], wq[k][1][:], w_bf16[k][:].rearrange("p n t -> p (n t)"))
 
         a = []
         for q in range(4):
             bank = ps.tile([P, LANES, QUARTER], F32, name="a%d" % q, tag="acc%d" % q)
             for j in range(LANES):
-                product(nc, bank[:, j, :], xq_d, cols(j, P), wq[q // 2], cols(q % 2, QUARTER))
+                product(nc, bank[:, j, :], xq_d, cols(j, P), wq[min(q, 2)], cols(max(q - 2, 0), QUARTER))
             a.append(bank)
 
         y_sq = [sb.tile([P, LANES, QUARTER], F32, name="y_sq%d" % q) for q in range(4)]
         g_bf16 = [sb.tile([P, HALF * LANES], BF16, name="g_bf16_%d" % h, align_bytes=64) for h in range(2)]
         gq = operand("gq", SLOTS)
-        sums = [ps.tile([P, 2, HALF], F32, name="sums%d" % h, tag="turn%d" % h) for h in range(2)]
+        sums_second = ps.tile([P, 2, HALF], F32, name="sums_second", tag="turn1")
+        s_rows = [ps.tile([P, HALF], F32, name="s_first", tag="s_first")[:], sums_second[:, 1, :]]
+        turned_tags = ("turn0", "acc0")
+        y_sq_turned = {}
         spent = sb.tile([P, SLOTS], F32, name="spent")
-        s_cols = [sb.tile([P, 2], F32, name="s_cols%d" % h) for h in range(2)]
-        b = [ps.tile([P, SLOTS], F32, name="b%d" % t, tag="b%d" % t) for t in range(2)]
+        s_cols = [sb.tile([P, 1], F32, name="s_cols%d" % q) for q in range(4)]
+        b = [ps.tile([P, SLOTS], F32, name="b0", tag="b0")]
         hebb = [sb.tile([P, SLOTS], F32, name="hebb%d" % t) for t in range(LANES)]
         decay = sb.tile([P, LANES, SLOTS], F32, name="decay")
 
@@ -154,32 +166,34 @@ def tile_attend_goja_pl_kernel(tc, xT, wT, us, fd, offs, out_0, out_1, out_2):
             )
 
         def turn_squares(q):
+            if q < 2:
+                y_sq_turned[q] = ps.tile([P, P], F32, name="y_sq_turned%d" % q, tag=turned_tags[q])[:]
+            else:
+                y_sq_turned[q] = sums_second[:, 0, cols(q % 2, P)]
             for j in range(LANES):
                 nc.tensor.matmul(
-                    sums[q // 2][:, 0, cols(q % 2, P)], y_sq[q][:, j, :], ident[:],
+                    y_sq_turned[q], y_sq[q][:, j, :], ident[:],
                     start=(j == 0), stop=(j == LANES - 1), is_transpose=True,
                 )
 
-        def sum_squares(h):
-            for k in range(2):
-                nc.scalar.activation(
-                    out=spent[:, cols(2 * h + k, P)], in_=sums[h][:, 0, cols(k, P)], func=COPY, accum_out=s_cols[h][:, k : k + 1]
-                )
+        def sum_squares(q):
+            nc.scalar.activation(out=spent[:, cols(q, P)], in_=y_sq_turned[q], func=COPY, accum_out=s_cols[q][:])
 
         def spread(q):
-            column = s_cols[q // 2][:, q % 2 : q % 2 + 1]
-            nc.tensor.transpose(sums[q // 2][:, 1, cols(q % 2, QUARTER)], column.to_broadcast([P, P]), ident[:])
+            nc.tensor.transpose(s_rows[q // 2][:, cols(q % 2, QUARTER)], s_cols[q][:].to_broadcast([P, P]), ident[:])
 
         def scale_b(t, bank, span):
             nc.scalar.activation(out=hebb[t][:, span], in_=bank[:, span], func=COPY, scale=fd_sq[:, t : t + 1])
 
-        def make_decay(planes, h):
-            count = planes.stop - planes.start
+        def make_decay(planes, span):
+            h = span.start // HALF
+            inside = slice(span.start - h * HALF, span.stop - h * HALF)
+            shape = [P, planes.stop - planes.start, span.stop - span.start]
             nc.vector.scalar_tensor_tensor(
-                out=decay[:, planes, cols(h, HALF)],
-                in0=sums[h][:, 1:2, :].to_broadcast([P, count, HALF]),
+                out=decay[:, planes, span],
+                in0=s_rows[h][:, inside].unsqueeze(1).to_broadcast(shape),
                 scalar=-1.0,
-                in1=w[h][:, planes, :],
+                in1=w[h][:, planes, inside],
                 op0=MULT,
                 op1=MULT,
             )
@@ -190,27 +204,31 @@ def tile_attend_goja_pl_kernel(tc, xT, wT, us, fd, offs, out_0, out_1, out_2):
 
         first, second = cols(0, HALF), cols(1, HALF)
         make_g(0)
-        square(1)
-        square(0)
-        make_g(2)
         make_g(1)
-        turn_squares(1)
-        turn_squares(0)
-        make_g(3)
+        make_g(2)
         quantize(nc, gq[0][:, first], gq[1][:, first], g_bf16[0][:])
-        sum_squares(0)
+        make_g(3)
+        square(0)
+        square(1)
+        turn_squares(0)
         product(nc, b[0][:, first], xq_r, cols(0, P), gq, first)
-        for q in (0, 1):
-            spread(q)
+        sum_squares(0)
+        spread(0)
         scale_b(0, b[0], first)
+        turn_squares(1)
+        make_decay(slice(0, 1), cols(0, QUARTER))
         quantize(nc, gq[0][:, second], gq[1][:, second], g_bf16[1][:])
-        make_decay(slice(0, 1), 0)
+        sum_squares(1)
+        spread(1)
+        scatter(0, cols(0, QUARTER))
         for q in (2, 3):
             square(q)
             turn_squares(q)
-        scatter(0, first)
-        make_decay(slice(1, 2), 0)
-        sum_squares(1)
+        make_decay(slice(0, 1), cols(1, QUARTER))
+        make_decay(slice(1, 2), first)
+        scatter(0, cols(1, QUARTER))
+        for q in (2, 3):
+            sum_squares(q)
         product(nc, b[0][:, second], xq_r, cols(0, P), gq, second)
         scale_b(0, b[0], second)
         for q in (2, 3):
@@ -218,8 +236,7 @@ def tile_attend_goja_pl_kernel(tc, xT, wT, us, fd, offs, out_0, out_1, out_2):
 
         whole = slice(0, SLOTS)
         for t in range(1, LANES):
-            if t > 1:
-                b.append(ps.tile([P, SLOTS], F32, name="b%d" % t, tag="acc%d" % t))
+            b.append(ps.tile([P, SLOTS], F32, name="b%d" % t, tag="acc%d" % t))
             product(nc, b[t][:], xq_r, cols(t, P), gq, whole)
             scale_b(t, b[t], whole)
 
@@ -233,11 +250,11 @@ def tile_attend_goja_pl_kernel(tc, xT, wT, us, fd, offs, out_0, out_1, out_2):
             for k, span in enumerate(spans):
                 nc.scalar.copy(out=pairs[k][:, t // 2, :, t % 2], in_=moved[t][:, span])
 
-        make_decay(slice(0, 2), 1)
+        make_decay(slice(0, 2), second)
         for t in range(LANES):
             if 0 < t < LANES - 1:
                 for h in range(2):
-                    make_decay(slice(t + 1, t + 2), h)
+                    make_decay(slice(t + 1, t + 2), cols(h, HALF))
             scatter(t, second if t == 0 else whole)
             finish_plane(t)
 

@@ -22,8 +22,18 @@ P = 128
 LANES = 4
 HALF = SLOTS // 2
 QUARTER = SLOTS // 4
-CHUNKS = ((128, 128, 256), (256, 256), (256, 256), (128, 256), (128,))
-SCALAR_WOVEN = 2
+PER_COLUMN = 16
+
+VECTOR_QUARTER = 3
+QUARTER_ORDER = (0, 1, 3, 2)
+
+CHUNK_GROUPS = ((128, 128, 256), (256, 256), (256, 256), (128, 256), (128,))
+SCALAR_WOVEN = 3
+VECTOR_ROUNDED = 2
+
+
+def cols(index, width):
+    return slice(index * width, (index + 1) * width)
 
 
 def quantize(nc, codes, scales, values):
@@ -42,10 +52,6 @@ def product(nc, out, left, left_cols, right, right_cols):
     )
 
 
-def cols(index, width):
-    return slice(index * width, (index + 1) * width)
-
-
 def tile_attend_goja_pl_kernel(tc, xT, wT, us, fd, offs, out_0, out_1, out_2):
     nc = tc.nc
     with ExitStack() as ctx:
@@ -60,7 +66,7 @@ def tile_attend_goja_pl_kernel(tc, xT, wT, us, fd, offs, out_0, out_1, out_2):
 
         x_f32 = sb.tile([P, LANES, R], F32, name="x_f32")
         nc.sync.dma_start(out=x_f32[:], in_=xT.rearrange("(p t) r -> p t r", t=LANES))
-        offsets = sb.tile([P, SLOTS // 16], U16, name="offsets")
+        offsets = sb.tile([P, SLOTS // PER_COLUMN], U16, name="offsets")
         nc.sync.dma_start(offsets[:], offs)
         table = []
         for t in range(LANES):
@@ -71,6 +77,9 @@ def tile_attend_goja_pl_kernel(tc, xT, wT, us, fd, offs, out_0, out_1, out_2):
         nc.scalar.dma_start(out=us_col[:], in_=us.rearrange("(p t) o -> p (t o)", t=LANES))
         fd_col = sb.tile([P, LANES], F32, name="fd_col")
         nc.scalar.dma_start(out=fd_col[:], in_=fd.rearrange("(p t) o -> p (t o)", t=LANES))
+
+        def list_slice(span):
+            return offsets[:, span.start // PER_COLUMN : span.stop // PER_COLUMN]
 
         ident = sb.tile([P, P], F32, name="ident")
         make_identity(nc, ident[:])
@@ -98,56 +107,51 @@ def tile_attend_goja_pl_kernel(tc, xT, wT, us, fd, offs, out_0, out_1, out_2):
         x_words = x_bf16[:].bitcast(F32)
         x_by_r = sb.tile([P, D * LANES], BF16, name="x_by_r", align_bytes=64)
         x_by_r_words = x_by_r[:].bitcast(F32).rearrange("s (t p u) -> s t p u", t=LANES, u=2)
-        for h in range(2):
-            turned = ps.tile([P, 2, 2, P], F32, name="turned%d" % h, tag="turn%d" % h)
-            for tt in range(2):
-                t = 2 * h + tt
+        plane_words = R // 2
+        for pair in range(2):
+            x_turned = ps.tile([P, 2, 2, P], F32, name="x_turned%d" % pair, tag="turn%d" % pair)
+            for e in range(2):
+                t = 2 * pair + e
                 for u in range(2):
-                    nc.tensor.transpose(turned[:, tt, u, :], x_words[:, 256 * t + u : 256 * (t + 1) : 2], ident[:])
-            nc.scalar.copy(out=x_by_r_words[:, 2 * h : 2 * h + 2], in_=turned[:].rearrange("s t u p -> s t p u"))
+                    every_second = x_words[:, plane_words * t + u : plane_words * (t + 1) : 2]
+                    nc.tensor.transpose(x_turned[:, e, u, :], every_second, ident[:])
+            nc.scalar.copy(out=x_by_r_words[:, cols(pair, 2)], in_=x_turned[:].rearrange("s t u p -> s t p u"))
         xq_r = operand("xq_r", D)
 
         w = [sb.tile([P, LANES, HALF], F32, name="w%d" % h) for h in range(2)]
-        pieces = (cols(0, QUARTER), cols(1, QUARTER), cols(1, HALF))
-        w_bf16 = [
-            sb.tile([P, piece.stop - piece.start, LANES], BF16, name="w_bf16_%d" % k, align_bytes=64)
-            for k, piece in enumerate(pieces)
-        ]
-        wq = [operand("wq%d" % k, piece.stop - piece.start) for k, piece in enumerate(pieces)]
+        w_bf16 = [sb.tile([P, QUARTER, LANES], BF16, name="w_bf16_%d" % q, align_bytes=64) for q in range(4)]
+        wq = [operand("wq%d" % q, QUARTER) for q in range(4)]
 
-        def round_w(copy, k, lanes):
-            h = pieces[k].start // HALF
-            inside = slice(pieces[k].start - h * HALF, pieces[k].stop - h * HALF)
-            copy(out=w_bf16[k][:, :, lanes], in_=w[h][:, lanes, inside].rearrange("p t n -> p n t"))
+        def round_w(copy, q, lanes):
+            copy(out=w_bf16[q][:, :, lanes], in_=w[q // 2][:, lanes, cols(q % 2, QUARTER)].rearrange("p t n -> p n t"))
 
         for t in range(LANES):
             for h in range(2):
-                nc.vector.tensor_copy(w[h][:, t, :], table[t][:].indirect(offsets[:, cols(h, HALF // 16)]))
+                nc.vector.tensor_copy(w[h][:, t, :], table[t][:].indirect(list_slice(cols(h, HALF))))
             if t == 0:
                 quantize(nc, xq_d[0][:], xq_d[1][:], x_by_d[:])
             if t == 1:
                 quantize(nc, xq_r[0][:], xq_r[1][:], x_by_r[:])
-                for k in range(len(pieces)):
-                    round_w(nc.scalar.copy, k, slice(0, 2))
-        for k in range(len(pieces)):
-            round_w(nc.scalar.copy if k < 2 else nc.vector.tensor_copy, k, slice(2, 4))
-            quantize(nc, wq[k][0][:], wq[k][1][:], w_bf16[k][:].rearrange("p n t -> p (n t)"))
+                for q in range(4):
+                    round_w(nc.scalar.copy, q, slice(0, 2))
+        for q in QUARTER_ORDER:
+            round_w(nc.vector.tensor_copy if q == VECTOR_QUARTER else nc.scalar.copy, q, slice(2, 4))
+            quantize(nc, wq[q][0][:], wq[q][1][:], w_bf16[q][:].rearrange("p n t -> p (n t)"))
 
-        a = []
-        for q in range(4):
-            bank = ps.tile([P, LANES, QUARTER], F32, name="a%d" % q, tag="acc%d" % q)
+        a = {}
+        for q in QUARTER_ORDER:
+            a[q] = ps.tile([P, LANES, QUARTER], F32, name="a%d" % q, tag="acc%d" % q)
             for j in range(LANES):
-                product(nc, bank[:, j, :], xq_d, cols(j, P), wq[min(q, 2)], cols(max(q - 2, 0), QUARTER))
-            a.append(bank)
+                product(nc, a[q][:, j, :], xq_d, cols(j, P), wq[q], slice(0, QUARTER))
 
         y_sq = [sb.tile([P, LANES, QUARTER], F32, name="y_sq%d" % q) for q in range(4)]
         g_bf16 = [sb.tile([P, HALF * LANES], BF16, name="g_bf16_%d" % h, align_bytes=64) for h in range(2)]
         gq = operand("gq", SLOTS)
         sums_second = ps.tile([P, 2, HALF], F32, name="sums_second", tag="turn1")
         s_rows = [ps.tile([P, HALF], F32, name="s_first", tag="s_first")[:], sums_second[:, 1, :]]
-        turned_tags = ("turn0", "acc0")
+        y_sq_tags = ("turn0", "acc0")
         y_sq_turned = {}
-        spent = sb.tile([P, SLOTS], F32, name="spent")
+        summands = sb.tile([P, SLOTS], F32, name="summands")
         s_cols = [sb.tile([P, 1], F32, name="s_cols%d" % q) for q in range(4)]
         b = [ps.tile([P, SLOTS], F32, name="b0", tag="b0")]
         hebb = [sb.tile([P, SLOTS], F32, name="hebb%d" % t) for t in range(LANES)]
@@ -166,8 +170,8 @@ def tile_attend_goja_pl_kernel(tc, xT, wT, us, fd, offs, out_0, out_1, out_2):
             )
 
         def turn_squares(q):
-            if q < 2:
-                y_sq_turned[q] = ps.tile([P, P], F32, name="y_sq_turned%d" % q, tag=turned_tags[q])[:]
+            if q < len(y_sq_tags):
+                y_sq_turned[q] = ps.tile([P, P], F32, name="y_sq_turned%d" % q, tag=y_sq_tags[q])[:]
             else:
                 y_sq_turned[q] = sums_second[:, 0, cols(q % 2, P)]
             for j in range(LANES):
@@ -177,13 +181,13 @@ def tile_attend_goja_pl_kernel(tc, xT, wT, us, fd, offs, out_0, out_1, out_2):
                 )
 
         def sum_squares(q):
-            nc.scalar.activation(out=spent[:, cols(q, P)], in_=y_sq_turned[q], func=COPY, accum_out=s_cols[q][:])
+            nc.scalar.activation(out=summands[:, cols(q, P)], in_=y_sq_turned[q], func=COPY, accum_out=s_cols[q][:])
 
         def spread(q):
             nc.tensor.transpose(s_rows[q // 2][:, cols(q % 2, QUARTER)], s_cols[q][:].to_broadcast([P, P]), ident[:])
 
-        def scale_b(t, bank, span):
-            nc.scalar.activation(out=hebb[t][:, span], in_=bank[:, span], func=COPY, scale=fd_sq[:, t : t + 1])
+        def scale_b(t, span):
+            nc.scalar.activation(out=hebb[t][:, span], in_=b[t][:, span], func=COPY, scale=fd_sq[:, t : t + 1])
 
         def make_decay(planes, span):
             h = span.start // HALF
@@ -199,29 +203,28 @@ def tile_attend_goja_pl_kernel(tc, xT, wT, us, fd, offs, out_0, out_1, out_2):
             )
 
         def scatter(t, span):
-            lists = offsets[:, span.start // 16 : span.stop // 16]
-            nc.vector.tensor_tensor(moved[t][:].indirect(lists), hebb[t][:, span], decay[:, t, span], ADD)
+            nc.vector.tensor_tensor(moved[t][:].indirect(list_slice(span)), hebb[t][:, span], decay[:, t, span], ADD)
 
-        first, second = cols(0, HALF), cols(1, HALF)
+        first, second, whole = cols(0, HALF), cols(1, HALF), slice(0, SLOTS)
         make_g(0)
         make_g(1)
-        make_g(2)
-        quantize(nc, gq[0][:, first], gq[1][:, first], g_bf16[0][:])
         make_g(3)
+        quantize(nc, gq[0][:, first], gq[1][:, first], g_bf16[0][:])
+        make_g(2)
         square(0)
         square(1)
         turn_squares(0)
         product(nc, b[0][:, first], xq_r, cols(0, P), gq, first)
         sum_squares(0)
         spread(0)
-        scale_b(0, b[0], first)
+        scale_b(0, first)
         turn_squares(1)
         make_decay(slice(0, 1), cols(0, QUARTER))
         quantize(nc, gq[0][:, second], gq[1][:, second], g_bf16[1][:])
         sum_squares(1)
         spread(1)
         scatter(0, cols(0, QUARTER))
-        for q in (2, 3):
+        for q in QUARTER_ORDER[2:]:
             square(q)
             turn_squares(q)
         make_decay(slice(0, 1), cols(1, QUARTER))
@@ -230,25 +233,24 @@ def tile_attend_goja_pl_kernel(tc, xT, wT, us, fd, offs, out_0, out_1, out_2):
         for q in (2, 3):
             sum_squares(q)
         product(nc, b[0][:, second], xq_r, cols(0, P), gq, second)
-        scale_b(0, b[0], second)
+        scale_b(0, second)
         for q in (2, 3):
             spread(q)
 
-        whole = slice(0, SLOTS)
         for t in range(1, LANES):
             b.append(ps.tile([P, SLOTS], F32, name="b%d" % t, tag="acc%d" % t))
             product(nc, b[t][:], xq_r, cols(t, P), gq, whole)
-            scale_b(t, b[t], whole)
+            scale_b(t, whole)
 
-        widths = [width for group in CHUNKS for width in group]
+        widths = [width for group in CHUNK_GROUPS for width in group]
         spans = [slice(sum(widths[:k]), sum(widths[: k + 1])) for k in range(len(widths))]
         pairs = [sb.tile([P, 2, width, 2], BF16, name="pairs%d" % k) for k, width in enumerate(widths)]
         out_rows = out_0.rearrange("(p t) c -> p t c", t=LANES)
 
         def finish_plane(t):
             nc.sync.dma_start(out=out_rows[:, t, :], in_=moved[t][:])
-            for k, span in enumerate(spans):
-                nc.scalar.copy(out=pairs[k][:, t // 2, :, t % 2], in_=moved[t][:, span])
+            for k in range(VECTOR_ROUNDED if t >= 2 else 0, len(spans)):
+                nc.scalar.copy(out=pairs[k][:, t // 2, :, t % 2], in_=moved[t][:, spans[k]])
 
         make_decay(slice(0, 2), second)
         for t in range(LANES):
@@ -257,34 +259,28 @@ def tile_attend_goja_pl_kernel(tc, xT, wT, us, fd, offs, out_0, out_1, out_2):
                     make_decay(slice(t + 1, t + 2), cols(h, HALF))
             scatter(t, second if t == 0 else whole)
             finish_plane(t)
+        for t in range(2, LANES):
+            for k in range(VECTOR_ROUNDED):
+                nc.vector.tensor_copy(out=pairs[k][:, t // 2, :, t % 2], in_=moved[t][:, spans[k]])
 
         y_scales = sb.tile([P, UNITS], U8, name="y_scales", align_bytes=64)
-        y_codes = [sb.tile([P, sum(group)], U32, name="y_codes%d" % m, align_bytes=64) for m, group in enumerate(CHUNKS)]
+        y_codes = [
+            sb.tile([P, sum(group)], U32, name="y_codes%d" % m, align_bytes=64) for m, group in enumerate(CHUNK_GROUPS)
+        ]
         woven = [sb.tile([P, width * LANES], BF16, name="woven%d" % k, align_bytes=64) for k, width in enumerate(widths)]
         out_words = out_1[0].rearrange("p c l -> p (c l)").bitcast(I32)
 
         def weave(k):
-            if k >= len(widths) - SCALAR_WOVEN:
-                nc.scalar.copy(
-                    out=woven[k][:].bitcast(U32).rearrange("p (c i u) -> p c u i", i=2, u=2),
-                    in_=pairs[k][:].rearrange("p u c e -> p (u c e)").bitcast(U32).rearrange("p (u c i) -> p c u i", u=2, i=2),
-                )
-            else:
-                nc.vector.tensor_copy(
-                    out=woven[k][:].bitcast(I32).rearrange("p (c i u) -> p c u i", i=2, u=2),
-                    in_=pairs[k][:].rearrange("p u c e -> p (u c e)").bitcast(I32).rearrange("p (u c i) -> p c u i", u=2, i=2),
-                )
-
-        def store_scales(span, queues):
-            for quad in range(4):
-                queues[quad % len(queues)].dma_start(
-                    out=out_2[0, 4 * quad : 4 * quad + 4, span].bitcast(I32),
-                    in_=y_scales[32 * quad : 32 * quad + 4, span].bitcast(I32),
-                )
+            copy, word = (nc.scalar.copy, U32) if k >= len(widths) - SCALAR_WOVEN else (nc.vector.tensor_copy, I32)
+            source = pairs[k][:].rearrange("p u c e -> p (u c e)").bitcast(word)
+            copy(
+                out=woven[k][:].bitcast(word).rearrange("p (c i u) -> p c u i", i=2, u=2),
+                in_=source.rearrange("p (u c i) -> p c u i", u=2, i=2),
+            )
 
         weave(0)
         k = 0
-        for m, group in enumerate(CHUNKS):
+        for m, group in enumerate(CHUNK_GROUPS):
             base = spans[k].start
             for width in group:
                 if k + 1 < len(widths):
@@ -293,4 +289,8 @@ def tile_attend_goja_pl_kernel(tc, xT, wT, us, fd, offs, out_0, out_1, out_2):
                 quantize(nc, y_codes[m][:, start : start + width], y_scales[:, spans[k]], woven[k][:])
                 k = k + 1
             nc.sync.dma_start(out=out_words[:, base : base + sum(group)], in_=y_codes[m][:].bitcast(I32))
-        store_scales(slice(0, UNITS), [nc.scalar, nc.sync])
+        for quad in range(4):
+            (nc.scalar if quad % 2 == 0 else nc.sync).dma_start(
+                out=out_2[0, 4 * quad : 4 * quad + 4, :].bitcast(I32),
+                in_=y_scales[32 * quad : 32 * quad + 4, :].bitcast(I32),
+            )

from contextlib import ExitStack

import concourse.mybir as mybir
from concourse.masks import make_identity

D, R, SLOTS, UNITS = 512, 512, 512, 2048
FLOPS = 2 * 2 * D * R * SLOTS

F32 = mybir.dt.float32
BF16 = mybir.dt.bfloat16
I32 = mybir.dt.int32
U32 = mybir.dt.uint32
U16 = mybir.dt.uint16
U8 = mybir.dt.uint8
FP8X4 = mybir.dt.float8_e4m3fn_x4
MULT = mybir.AluOpType.mult
ADD = mybir.AluOpType.add
COPY = mybir.ActivationFunctionType.Copy
SQUARE = mybir.ActivationFunctionType.Square

P = 128
LANES = 4
HALF = SLOTS // 2
QUARTER = SLOTS // 4
PER_COLUMN = 16

VECTOR_QUARTER = 3
QUARTER_ORDER = (0, 1, 3, 2)

CHUNK_GROUPS = ((128, 128, 256), (256, 256), (256, 256), (128, 256), (128,))
SCALAR_WOVEN = 3
VECTOR_ROUNDED = 2


def cols(index, width):
    return slice(index * width, (index + 1) * width)


def quantize(nc, codes, scales, values):
    nc.vector.quantize_mx(out=codes.bitcast(FP8X4), scales=scales, in_=values)


def product(nc, out, left, left_cols, right, right_cols):
    nc.tensor.matmul_mx(
        out=out,
        lhsT=left[0][:, left_cols].bitcast(FP8X4),
        lhsT_scale=left[1][:, left_cols],
        rhs=right[0][:, right_cols].bitcast(FP8X4),
        rhs_scale=right[1][:, right_cols],
        start=True,
        stop=True,
    )


def tile_attend_goja_pl_kernel(tc, xT, wT, us, fd, offs, out_0, out_1, out_2):
    nc = tc.nc
    with ExitStack() as ctx:
        sb = ctx.enter_context(tc.tile_pool(name="sb", bufs=1))
        ps = ctx.enter_context(tc.psum_pool(name="ps", bufs=1))

        def operand(name, width):
            return (
                sb.tile([P, width], U32, name=name + "_codes", align_bytes=64),
                sb.tile([P, width], U8, name=name + "_scales", align_bytes=64),
            )

        x_f32 = sb.tile([P, LANES, R], F32, name="x_f32")
        nc.sync.dma_start(out=x_f32[:], in_=xT.rearrange("(p t) r -> p t r", t=LANES))
        offsets = sb.tile([P, SLOTS // PER_COLUMN], U16, name="offsets")
        nc.sync.dma_start(offsets[:], offs)
        table = []
        for t in range(LANES):
            plane = sb.tile([P, UNITS], F32, name="table%d" % t)
            nc.sync.dma_start(out=plane[:], in_=wT.rearrange("(p t) c -> p t c", t=LANES)[:, t, :])
            table.append(plane)
        us_col = sb.tile([P, LANES], F32, name="us_col")
        nc.scalar.dma_start(out=us_col[:], in_=us.rearrange("(p t) o -> p (t o)", t=LANES))
        fd_col = sb.tile([P, LANES], F32, name="fd_col")
        nc.scalar.dma_start(out=fd_col[:], in_=fd.rearrange("(p t) o -> p (t o)", t=LANES))

        def list_slice(span):
            return offsets[:, span.start // PER_COLUMN : span.stop // PER_COLUMN]

        ident = sb.tile([P, P], F32, name="ident")
        make_identity(nc, ident[:])

        moved = []
        for t in range(LANES):
            window = sb.tile([P, UNITS], F32, name="moved%d" % t)
            nc.vector.memset(window[:], 0.0)
            moved.append(window)

        us_sq = sb.tile([P, LANES], F32, name="us_sq")
        nc.scalar.activation(out=us_sq[:], in_=us_col[:], func=SQUARE)
        fd_sq = sb.tile([P, LANES], F32, name="fd_sq")
        nc.scalar.activation(out=fd_sq[:], in_=fd_col[:], func=SQUARE)

        x_by_d = sb.tile([P, R * LANES], BF16, name="x_by_d", align_bytes=64)
        nc.vector.tensor_copy(
            out=x_by_d[:].rearrange("p (j s t) -> p s j t", j=LANES, t=LANES),
            in_=x_f32[:].rearrange("p t (s j) -> p s j t", j=LANES),
        )
        xq_d = operand("xq_d", R)

        x_bf16 = sb.tile([P, LANES * R], BF16, name="x_bf16")
        nc.scalar.copy(out=x_bf16[:], in_=x_f32[:].rearrange("p t r -> p (t r)"))
        x_words = x_bf16[:].bitcast(F32)
        x_by_r = sb.tile([P, D * LANES], BF16, name="x_by_r", align_bytes=64)
        x_by_r_words = x_by_r[:].bitcast(F32).rearrange("s (t p u) -> s t p u", t=LANES, u=2)
        plane_words = R // 2
        for pair in range(2):
            x_turned = ps.tile([P, 2, 2, P], F32, name="x_turned%d" % pair, tag="turn%d" % pair)
            for e in range(2):
                t = 2 * pair + e
                for u in range(2):
                    every_second = x_words[:, plane_words * t + u : plane_words * (t + 1) : 2]
                    nc.tensor.transpose(x_turned[:, e, u, :], every_second, ident[:])
            nc.scalar.copy(out=x_by_r_words[:, cols(pair, 2)], in_=x_turned[:].rearrange("s t u p -> s t p u"))
        xq_r = operand("xq_r", D)

        w = [sb.tile([P, LANES, HALF], F32, name="w%d" % h) for h in range(2)]
        w_bf16 = [sb.tile([P, QUARTER, LANES], BF16, name="w_bf16_%d" % q, align_bytes=64) for q in range(4)]
        wq = [operand("wq%d" % q, QUARTER) for q in range(4)]

        def round_w(copy, q, lanes):
            copy(out=w_bf16[q][:, :, lanes], in_=w[q // 2][:, lanes, cols(q % 2, QUARTER)].rearrange("p t n -> p n t"))

        for t in range(LANES):
            for h in range(2):
                nc.vector.tensor_copy(w[h][:, t, :], table[t][:].indirect(list_slice(cols(h, HALF))))
            if t == 0:
                quantize(nc, xq_d[0][:], xq_d[1][:], x_by_d[:])
            if t == 1:
                quantize(nc, xq_r[0][:], xq_r[1][:], x_by_r[:])
                for q in range(4):
                    round_w(nc.scalar.copy, q, slice(0, 2))
        for q in QUARTER_ORDER:
            round_w(nc.vector.tensor_copy if q == VECTOR_QUARTER else nc.scalar.copy, q, slice(2, 4))
            quantize(nc, wq[q][0][:], wq[q][1][:], w_bf16[q][:].rearrange("p n t -> p (n t)"))

        a = {}
        for q in QUARTER_ORDER:
            a[q] = ps.tile([P, LANES, QUARTER], F32, name="a%d" % q, tag="acc%d" % q)
            for j in range(LANES):
                product(nc, a[q][:, j, :], xq_d, cols(j, P), wq[q], slice(0, QUARTER))

        y_sq = [sb.tile([P, LANES, QUARTER], F32, name="y_sq%d" % q) for q in range(4)]
        g_bf16 = [sb.tile([P, HALF * LANES], BF16, name="g_bf16_%d" % h, align_bytes=64) for h in range(2)]
        gq = operand("gq", SLOTS)
        sums_second = ps.tile([P, 2, HALF], F32, name="sums_second", tag="turn1")
        s_rows = [ps.tile([P, HALF], F32, name="s_first", tag="s_first")[:], sums_second[:, 1, :]]
        y_sq_tags = ("turn0", "acc0")
        y_sq_turned = {}
        summands = sb.tile([P, SLOTS], F32, name="summands")
        s_cols = [sb.tile([P, 1], F32, name="s_cols%d" % q) for q in range(4)]
        b = [ps.tile([P, SLOTS], F32, name="b0", tag="b0")]
        hebb = [sb.tile([P, SLOTS], F32, name="hebb%d" % t) for t in range(LANES)]
        decay = sb.tile([P, LANES, SLOTS], F32, name="decay")

        def square(q):
            for j in range(LANES):
                nc.scalar.activation(out=y_sq[q][:, j, :], in_=a[q][:, j, :], func=SQUARE, scale=us_col[:, j : j + 1])

        def make_g(q):
            nc.vector.tensor_tensor(
                out=g_bf16[q // 2][:, cols(q % 2, QUARTER * LANES)].rearrange("s (n j) -> s n j", j=LANES),
                in0=a[q][:].rearrange("s j n -> s n j"),
                in1=us_sq[:].unsqueeze(1).to_broadcast([P, QUARTER, LANES]),
                op=MULT,
            )

        def turn_squares(q):
            if q < len(y_sq_tags):
                y_sq_turned[q] = ps.tile([P, P], F32, name="y_sq_turned%d" % q, tag=y_sq_tags[q])[:]
            else:
                y_sq_turned[q] = sums_second[:, 0, cols(q % 2, P)]
            for j in range(LANES):
                nc.tensor.matmul(
                    y_sq_turned[q], y_sq[q][:, j, :], ident[:],
                    start=(j == 0), stop=(j == LANES - 1), is_transpose=True,
                )

        def sum_squares(q):
            nc.scalar.activation(out=summands[:, cols(q, P)], in_=y_sq_turned[q], func=COPY, accum_out=s_cols[q][:])

        def spread(q):
            nc.tensor.transpose(s_rows[q // 2][:, cols(q % 2, QUARTER)], s_cols[q][:].to_broadcast([P, P]), ident[:])

        def scale_b(t, span):
            nc.scalar.activation(out=hebb[t][:, span], in_=b[t][:, span], func=COPY, scale=fd_sq[:, t : t + 1])

        def make_decay(planes, span):
            h = span.start // HALF
            inside = slice(span.start - h * HALF, span.stop - h * HALF)
            shape = [P, planes.stop - planes.start, span.stop - span.start]
            nc.vector.scalar_tensor_tensor(
                out=decay[:, planes, span],
                in0=s_rows[h][:, inside].unsqueeze(1).to_broadcast(shape),
                scalar=-1.0,
                in1=w[h][:, planes, inside],
                op0=MULT,
                op1=MULT,
            )

        def scatter(t, span):
            nc.vector.tensor_tensor(moved[t][:].indirect(list_slice(span)), hebb[t][:, span], decay[:, t, span], ADD)

        first, second, whole = cols(0, HALF), cols(1, HALF), slice(0, SLOTS)
        make_g(0)
        make_g(1)
        make_g(3)
        quantize(nc, gq[0][:, first], gq[1][:, first], g_bf16[0][:])
        make_g(2)
        square(0)
        square(1)
        turn_squares(0)
        product(nc, b[0][:, first], xq_r, cols(0, P), gq, first)
        sum_squares(0)
        spread(0)
        scale_b(0, first)
        turn_squares(1)
        make_decay(slice(0, 1), cols(0, QUARTER))
        quantize(nc, gq[0][:, second], gq[1][:, second], g_bf16[1][:])
        sum_squares(1)
        spread(1)
        scatter(0, cols(0, QUARTER))
        for q in QUARTER_ORDER[2:]:
            square(q)
            turn_squares(q)
        make_decay(slice(0, 1), cols(1, QUARTER))
        make_decay(slice(1, 2), first)
        scatter(0, cols(1, QUARTER))
        for q in (2, 3):
            sum_squares(q)
        product(nc, b[0][:, second], xq_r, cols(0, P), gq, second)
        scale_b(0, second)
        for q in (2, 3):
            spread(q)

        for t in range(1, LANES):
            b.append(ps.tile([P, SLOTS], F32, name="b%d" % t, tag="acc%d" % t))
            product(nc, b[t][:], xq_r, cols(t, P), gq, whole)
            scale_b(t, whole)

        widths = [width for group in CHUNK_GROUPS for width in group]
        spans = [slice(sum(widths[:k]), sum(widths[: k + 1])) for k in range(len(widths))]
        pairs = [sb.tile([P, 2, width, 2], BF16, name="pairs%d" % k) for k, width in enumerate(widths)]
        out_rows = out_0.rearrange("(p t) c -> p t c", t=LANES)

        def finish_plane(t):
            nc.sync.dma_start(out=out_rows[:, t, :], in_=moved[t][:])
            for k in range(VECTOR_ROUNDED if t >= 2 else 0, len(spans)):
                nc.scalar.copy(out=pairs[k][:, t // 2, :, t % 2], in_=moved[t][:, spans[k]])

        make_decay(slice(0, 2), second)
        for t in range(LANES):
            if 0 < t < LANES - 1:
                for h in range(2):
                    make_decay(slice(t + 1, t + 2), cols(h, HALF))
            scatter(t, second if t == 0 else whole)
            finish_plane(t)
        for t in range(2, LANES):
            for k in range(VECTOR_ROUNDED):
                nc.vector.tensor_copy(out=pairs[k][:, t // 2, :, t % 2], in_=moved[t][:, spans[k]])

        y_scales = sb.tile([P, UNITS], U8, name="y_scales", align_bytes=64)
        y_codes = [
            sb.tile([P, sum(group)], U32, name="y_codes%d" % m, align_bytes=64) for m, group in enumerate(CHUNK_GROUPS)
        ]
        woven = [sb.tile([P, width * LANES], BF16, name="woven%d" % k, align_bytes=64) for k, width in enumerate(widths)]
        out_words = out_1[0].rearrange("p c l -> p (c l)").bitcast(I32)

        def weave(k):
            copy, word = (nc.scalar.copy, U32) if k >= len(widths) - SCALAR_WOVEN else (nc.vector.tensor_copy, I32)
            source = pairs[k][:].rearrange("p u c e -> p (u c e)").bitcast(word)
            copy(
                out=woven[k][:].bitcast(word).rearrange("p (c i u) -> p c u i", i=2, u=2),
                in_=source.rearrange("p (u c i) -> p c u i", u=2, i=2),
            )

        weave(0)
        k = 0
        for m, group in enumerate(CHUNK_GROUPS):
            base = spans[k].start
            for width in group:
                if k + 1 < len(widths):
                    weave(k + 1)
                start = spans[k].start - base
                quantize(nc, y_codes[m][:, start : start + width], y_scales[:, spans[k]], woven[k][:])
                k = k + 1
            nc.sync.dma_start(out=out_words[:, base : base + sum(group)], in_=y_codes[m][:].bitcast(I32))
        for quad in range(4):
            (nc.scalar if quad % 2 == 0 else nc.sync).dma_start(
                out=out_2[0, 4 * quad : 4 * quad + 4, :].bitcast(I32),
                in_=y_scales[32 * quad : 32 * quad + 4, :].bitcast(I32),
            )
